import numpy as np
CORES = [114,242,370,498]
N = 4
ROOT = 3
def setup_inputs(rng):
    return {"x": rng.standard_normal((N, 128, 256), dtype=np.float32)}
def reference(x):
    y = np.full((N, 128, N * 256), np.nan, x.dtype)
    y[ROOT] = np.concatenate(list(x), axis=1)
    return {"y": y}

@@ -1,0 +1,80 @@
+from concourse.bass import RemoteDMATransfer, DstId
+
+C = 1
+S = 2 * C
+K = 1
+
+SCRATCH = {
+    "l0": ("dram", [K, 128, 256 // K], "float32"),
+    "l2": ("dram", [K, 128, 256 // K], "float32"),
+    "l1": ("dram", [S, 128, 256 // S], "float32"),
+}
+SEMAPHORES = ["ld0", "ld1", "ld2", "ld3", "st", "sent",
+              "a0", "a1", "a2", "a3", "b0", "b1", "b2", "b3",
+              "c0", "c1", "c2", "c3", "c4", "c5", "c6", "c7"]
+
+OFF_CHIP = 0xFF
+
+
+def rank_program(g, core, T, topo):
+    r0, r1, r2, root = T.cores
+    relay_a = root - 128 + 4
+    relay_b = r0 - 2
+    ld = [T.sem.ld0, T.sem.ld1, T.sem.ld2, T.sem.ld3]
+    sa = [T.sem.a0, T.sem.a1, T.sem.a2, T.sem.a3]
+    sb = [T.sem.b0, T.sem.b1, T.sem.b2, T.sem.b3]
+    sc = [T.sem.c0, T.sem.c1, T.sem.c2, T.sem.c3, T.sem.c4, T.sem.c5, T.sem.c6, T.sem.c7]
+
+    if core == r0 or core == r2:
+        buf, sems = (T.l0, sa) if core == r0 else (T.l2, sb)
+        rid, pid = topo.addr(root, core)
+        rows = 128 // K
+        for k in range(K):
+            g.dma_start(buf[k], T.x[k * rows:(k + 1) * rows, :]).then_inc(ld[k], 16)
+        for k in range(K):
+            g.wait_ge(ld[k], 16)
+            g.remote_dma(buf[k], buf[k], sems[k], T.sem.sent, pid, rid, OFF_CHIP)
+        g.wait_ge(T.sem.sent, 8 * K)
+
+    elif core == r1:
+        rows = 128 // S
+        ra, pa = topo.addr(relay_a, core)
+        rb, pb = topo.addr(relay_b, core)
+        for c in range(C):
+            g.dma_start(T.l1[2 * c:2 * c + 2], T.x[2 * c * rows:(2 * c + 2) * rows, :]).then_inc(ld[c], 16)
+        for c in range(C):
+            g.wait_ge(ld[c], 16)
+            g.remote_dma_fused([
+                RemoteDMATransfer(dst_ids=[DstId(rid=ra, pnc=pa)], dma_engine_mask=0x0F, remote_sem=sc[2 * c],
+                                  src=T.l1[2 * c], dst=T.l1[2 * c]),
+                RemoteDMATransfer(dst_ids=[DstId(rid=rb, pnc=pb)], dma_engine_mask=0xF0, remote_sem=sc[2 * c + 1],
+                                  src=T.l1[2 * c + 1], dst=T.l1[2 * c + 1]),
+            ], local_sem=T.sem.sent)
+        g.wait_ge(T.sem.sent, 8 * C)
+
+    elif core == relay_a or core == relay_b:
+        first = 0 if core == relay_a else 1
+        rid, pid = topo.addr(root, core)
+        for c in range(C):
+            t = 2 * c + first
+            g.wait_ge(sc[t], 4)
+            g.remote_dma(T.l1[t], T.l1[t], sc[t], T.sem.sent, pid, rid, OFF_CHIP)
+        g.wait_ge(T.sem.sent, 8 * C)
+
+    elif core == root:
+        n = 1
+        g.dma_start(T.y[:, 768:1024], T.x[:, :]).then_inc(T.sem.st, 16)
+        rows = 128 // K
+        for k in range(K):
+            g.wait_ge(sb[k], 8)
+            g.dma_start(T.y[k * rows:(k + 1) * rows, 512:768], T.l2[k]).then_inc(T.sem.st, 16)
+            g.wait_ge(sa[k], 8)
+            g.dma_start(T.y[k * rows:(k + 1) * rows, 0:256], T.l0[k]).then_inc(T.sem.st, 16)
+            n += 2
+        rows = 128 // S
+        for c in range(C):
+            g.wait_ge(sc[2 * c], 8)
+            g.wait_ge(sc[2 * c + 1], 8)
+            g.dma_start(T.y[2 * c * rows:(2 * c + 2) * rows, 256:512], T.l1[2 * c:2 * c + 2]).then_inc(T.sem.st, 16)
+            n += 1
+        g.wait_ge(T.sem.st, 16 * n)

@@ -1,17 +1,11 @@
 from concourse.bass import RemoteDMATransfer, DstId
 
-C = 1
-S = 2 * C
-K = 1
-
 SCRATCH = {
-    "l0": ("dram", [K, 128, 256 // K], "float32"),
-    "l2": ("dram", [K, 128, 256 // K], "float32"),
-    "l1": ("dram", [S, 128, 256 // S], "float32"),
+    "l0": ("dram", [2, 128, 128], "float32"),
+    "l2": ("dram", [128, 256], "float32"),
+    "l1": ("dram", [2, 128, 128], "float32"),
 }
-SEMAPHORES = ["ld0", "ld1", "ld2", "ld3", "st", "sent",
-              "a0", "a1", "a2", "a3", "b0", "b1", "b2", "b3",
-              "c0", "c1", "c2", "c3", "c4", "c5", "c6", "c7"]
+SEMAPHORES = ["ld", "st", "sent", "a0", "a1", "b0", "c0", "c1"]
 
 OFF_CHIP = 0xFF
 
@@ -20,61 +14,63 @@ def rank_program(g, core, T, topo):
     r0, r1, r2, root = T.cores
     relay_a = root - 128 + 4
     relay_b = r0 - 2
-    ld = [T.sem.ld0, T.sem.ld1, T.sem.ld2, T.sem.ld3]
-    sa = [T.sem.a0, T.sem.a1, T.sem.a2, T.sem.a3]
-    sb = [T.sem.b0, T.sem.b1, T.sem.b2, T.sem.b3]
-    sc = [T.sem.c0, T.sem.c1, T.sem.c2, T.sem.c3, T.sem.c4, T.sem.c5, T.sem.c6, T.sem.c7]
+    helper0 = r0 + 4
 
-    if core == r0 or core == r2:
-        buf, sems = (T.l0, sa) if core == r0 else (T.l2, sb)
+    if core == r2:
         rid, pid = topo.addr(root, core)
-        rows = 128 // K
-        for k in range(K):
-            g.dma_start(buf[k], T.x[k * rows:(k + 1) * rows, :]).then_inc(ld[k], 16)
-        for k in range(K):
-            g.wait_ge(ld[k], 16)
-            g.remote_dma(buf[k], buf[k], sems[k], T.sem.sent, pid, rid, OFF_CHIP)
-        g.wait_ge(T.sem.sent, 8 * K)
+        g.dma_start(T.l2[:, :], T.x[:, :]).then_inc(T.sem.ld, 16)
+        g.wait_ge(T.sem.ld, 16)
+        g.remote_dma(T.l2[:, :], T.l2[:, :], T.sem.b0, T.sem.sent, pid, rid, OFF_CHIP)
+        g.wait_ge(T.sem.sent, 8)
+
+    elif core == r0:
+        rr, pr = topo.addr(root, core)
+        rh, ph = topo.addr(helper0, core)
+        g.dma_start(T.l0[0:2], T.x[:, :]).then_inc(T.sem.ld, 16)
+        g.wait_ge(T.sem.ld, 16)
+        g.remote_dma_fused([
+            RemoteDMATransfer(dst_ids=[DstId(rid=rh, pnc=ph)], dma_engine_mask=0xFF00, remote_sem=T.sem.a1,
+                              src=T.l0[1], dst=T.l0[1]),
+            RemoteDMATransfer(dst_ids=[DstId(rid=rr, pnc=pr)], dma_engine_mask=0x00FF, remote_sem=T.sem.a0,
+                              src=T.l0[0], dst=T.l0[0]),
+        ], local_sem=T.sem.sent)
+        g.wait_ge(T.sem.sent, 16)
+
+    elif core == helper0:
+        rid, pid = topo.addr(root, core)
+        g.wait_ge(T.sem.a1, 8)
+        g.remote_dma(T.l0[1], T.l0[1], T.sem.a1, T.sem.sent, pid, rid, OFF_CHIP)
+        g.wait_ge(T.sem.sent, 8)
 
     elif core == r1:
-        rows = 128 // S
         ra, pa = topo.addr(relay_a, core)
         rb, pb = topo.addr(relay_b, core)
-        for c in range(C):
-            g.dma_start(T.l1[2 * c:2 * c + 2], T.x[2 * c * rows:(2 * c + 2) * rows, :]).then_inc(ld[c], 16)
-        for c in range(C):
-            g.wait_ge(ld[c], 16)
-            g.remote_dma_fused([
-                RemoteDMATransfer(dst_ids=[DstId(rid=ra, pnc=pa)], dma_engine_mask=0x0F, remote_sem=sc[2 * c],
-                                  src=T.l1[2 * c], dst=T.l1[2 * c]),
-                RemoteDMATransfer(dst_ids=[DstId(rid=rb, pnc=pb)], dma_engine_mask=0xF0, remote_sem=sc[2 * c + 1],
-                                  src=T.l1[2 * c + 1], dst=T.l1[2 * c + 1]),
-            ], local_sem=T.sem.sent)
-        g.wait_ge(T.sem.sent, 8 * C)
+        g.dma_start(T.l1[0:2], T.x[:, :]).then_inc(T.sem.ld, 16)
+        g.wait_ge(T.sem.ld, 16)
+        g.remote_dma_fused([
+            RemoteDMATransfer(dst_ids=[DstId(rid=ra, pnc=pa)], dma_engine_mask=0x0F, remote_sem=T.sem.c0,
+                              src=T.l1[0], dst=T.l1[0]),
+            RemoteDMATransfer(dst_ids=[DstId(rid=rb, pnc=pb)], dma_engine_mask=0xF0, remote_sem=T.sem.c1,
+                              src=T.l1[1], dst=T.l1[1]),
+        ], local_sem=T.sem.sent)
+        g.wait_ge(T.sem.sent, 8)
 
     elif core == relay_a or core == relay_b:
-        first = 0 if core == relay_a else 1
+        t, sem = (0, T.sem.c0) if core == relay_a else (1, T.sem.c1)
         rid, pid = topo.addr(root, core)
-        for c in range(C):
-            t = 2 * c + first
-            g.wait_ge(sc[t], 4)
-            g.remote_dma(T.l1[t], T.l1[t], sc[t], T.sem.sent, pid, rid, OFF_CHIP)
-        g.wait_ge(T.sem.sent, 8 * C)
+        g.wait_ge(sem, 4)
+        g.remote_dma(T.l1[t], T.l1[t], sem, T.sem.sent, pid, rid, OFF_CHIP)
+        g.wait_ge(T.sem.sent, 8)
 
     elif core == root:
-        n = 1
         g.dma_start(T.y[:, 768:1024], T.x[:, :]).then_inc(T.sem.st, 16)
-        rows = 128 // K
-        for k in range(K):
-            g.wait_ge(sb[k], 8)
-            g.dma_start(T.y[k * rows:(k + 1) * rows, 512:768], T.l2[k]).then_inc(T.sem.st, 16)
-            g.wait_ge(sa[k], 8)
-            g.dma_start(T.y[k * rows:(k + 1) * rows, 0:256], T.l0[k]).then_inc(T.sem.st, 16)
-            n += 2
-        rows = 128 // S
-        for c in range(C):
-            g.wait_ge(sc[2 * c], 8)
-            g.wait_ge(sc[2 * c + 1], 8)
-            g.dma_start(T.y[2 * c * rows:(2 * c + 2) * rows, 256:512], T.l1[2 * c:2 * c + 2]).then_inc(T.sem.st, 16)
-            n += 1
-        g.wait_ge(T.sem.st, 16 * n)
+        g.wait_ge(T.sem.b0, 8)
+        g.dma_start(T.y[:, 512:768], T.l2[:, :]).then_inc(T.sem.st, 16)
+        g.wait_ge(T.sem.a0, 8)
+        g.dma_start(T.y[0:64, 0:256], T.l0[0]).then_inc(T.sem.st, 16)
+        g.wait_ge(T.sem.a1, 8)
+        g.dma_start(T.y[64:128, 0:256], T.l0[1]).then_inc(T.sem.st, 16)
+        g.wait_ge(T.sem.c0, 8)
+        g.wait_ge(T.sem.c1, 8)
+        g.dma_start(T.y[:, 256:512], T.l1[0:2]).then_inc(T.sem.st, 16)
+        g.wait_ge(T.sem.st, 16 * 5)

@@ -1,76 +1,105 @@
 from concourse.bass import RemoteDMATransfer, DstId
 
-SCRATCH = {
-    "l0": ("dram", [2, 128, 128], "float32"),
-    "l2": ("dram", [128, 256], "float32"),
-    "l1": ("dram", [2, 128, 128], "float32"),
-}
-SEMAPHORES = ["ld", "st", "sent", "a0", "a1", "b0", "c0", "c1"]
+G = 16
+NG = 128 // G
 
-OFF_CHIP = 0xFF
+SCRATCH = {
+    "l0": ("dram", [NG, 128, 2 * G], "float32"),
+    "l1": ("dram", [NG, 128, 2 * G], "float32"),
+    "l2": ("dram", [128, 256], "float32"),
+}
+SEMAPHORES = ["ld", "st", "sent", "b0", "q0", "q1", "q2", "q3", "q4", "q5", "q6", "q7"]
+
+R0, R1, R2, ROOT = 114, 242, 370, 498
+H01, H45, H67 = R0 - 2, R0 + 2, R0 + 4
+RA = R2 + 4
+
+WAYS = [
+    (0, 0, 4, None),
+    (0, 4, 3, H67),
+    (0, 7, 1, H45),
+    (1, 0, 3, RA),
+    (1, 3, 3, H01),
+    (1, 6, 2, H45),
+]
+STORES = [
+    ([2, 0, 1], 0, 0, 8),
+    ([5, 3, 4], 1, 0, 8),
+]
+
+
+def share(n):
+    return {1: 8, 2: 4, 3: 2, 4: 2}.get(n, 1)
 
 
 def rank_program(g, core, T, topo):
-    r0, r1, r2, root = T.cores
-    relay_a = root - 128 + 4
-    relay_b = r0 - 2
-    helper0 = r0 + 4
+    q = [T.sem.q0, T.sem.q1, T.sem.q2, T.sem.q3, T.sem.q4, T.sem.q5, T.sem.q6, T.sem.q7]
+    img = [T.l0, T.l1]
 
-    if core == r2:
-        rid, pid = topo.addr(root, core)
+    def transfers(ways, dst_of, base):
+        n = sum(WAYS[i][2] for i in ways)
+        per = share(n)
+        out, e = [], base
+        for i in ways:
+            rank, g0, ng, relay = WAYS[i]
+            rid, pid = topo.addr(dst_of(i), core)
+            for k in range(g0, g0 + ng):
+                out.append(RemoteDMATransfer(dst_ids=[DstId(rid=rid, pnc=pid)], dma_engine_mask=((1 << per) - 1) << e,
+                                             remote_sem=q[i], src=img[rank][k], dst=img[rank][k]))
+                e += per
+        return out, per
+
+    def first_hop(i):
+        return WAYS[i][3] if WAYS[i][3] is not None else ROOT
+
+    def first_share(i):
+        rank = WAYS[i][0]
+        src = R0 if rank == 0 else R1
+        on = topo.mask(src, first_hop(i)) == 0xFFFF
+        return share(sum(w[2] for j, w in enumerate(WAYS)
+                         if w[0] == rank and (topo.mask(src, first_hop(j)) == 0xFFFF) == on))
+
+    if core == R2:
+        rid, pid = topo.addr(ROOT, core)
         g.dma_start(T.l2[:, :], T.x[:, :]).then_inc(T.sem.ld, 16)
         g.wait_ge(T.sem.ld, 16)
-        g.remote_dma(T.l2[:, :], T.l2[:, :], T.sem.b0, T.sem.sent, pid, rid, OFF_CHIP)
+        g.remote_dma(T.l2[:, :], T.l2[:, :], T.sem.b0, T.sem.sent, pid, rid, 0xFF)
         g.wait_ge(T.sem.sent, 8)
 
-    elif core == r0:
-        rr, pr = topo.addr(root, core)
-        rh, ph = topo.addr(helper0, core)
-        g.dma_start(T.l0[0:2], T.x[:, :]).then_inc(T.sem.ld, 16)
+    elif core == R0 or core == R1:
+        rank = 0 if core == R0 else 1
+        mine = [i for i, w in enumerate(WAYS) if w[0] == rank]
+        off = [i for i in mine if topo.mask(core, first_hop(i)) != 0xFFFF]
+        on = [i for i in mine if topo.mask(core, first_hop(i)) == 0xFFFF]
+        g.dma_start(img[rank][0:NG], T.x[:, :]).then_inc(T.sem.ld, 16)
         g.wait_ge(T.sem.ld, 16)
-        g.remote_dma_fused([
-            RemoteDMATransfer(dst_ids=[DstId(rid=rh, pnc=ph)], dma_engine_mask=0xFF00, remote_sem=T.sem.a1,
-                              src=T.l0[1], dst=T.l0[1]),
-            RemoteDMATransfer(dst_ids=[DstId(rid=rr, pnc=pr)], dma_engine_mask=0x00FF, remote_sem=T.sem.a0,
-                              src=T.l0[0], dst=T.l0[0]),
-        ], local_sem=T.sem.sent)
-        g.wait_ge(T.sem.sent, 16)
+        tr, per = transfers(off, first_hop, 0)
+        total = per * len(tr)
+        if on:
+            tr2, per2 = transfers(on, first_hop, 8)
+            total += per2 * len(tr2)
+            tr = tr2 + tr
+        g.remote_dma_fused(tr, local_sem=T.sem.sent)
+        g.wait_ge(T.sem.sent, total)
 
-    elif core == helper0:
-        rid, pid = topo.addr(root, core)
-        g.wait_ge(T.sem.a1, 8)
-        g.remote_dma(T.l0[1], T.l0[1], T.sem.a1, T.sem.sent, pid, rid, OFF_CHIP)
-        g.wait_ge(T.sem.sent, 8)
+    elif core in (H01, H45, H67, RA):
+        total = 0
+        for i, w in enumerate(WAYS):
+            if w[3] == core:
+                g.wait_ge(q[i], first_share(i) * w[2])
+                tr, per = transfers([i], lambda j: ROOT, 0)
+                g.remote_dma_fused(tr, local_sem=T.sem.sent)
+                total += per * len(tr)
+        g.wait_ge(T.sem.sent, total)
 
-    elif core == r1:
-        ra, pa = topo.addr(relay_a, core)
-        rb, pb = topo.addr(relay_b, core)
-        g.dma_start(T.l1[0:2], T.x[:, :]).then_inc(T.sem.ld, 16)
-        g.wait_ge(T.sem.ld, 16)
-        g.remote_dma_fused([
-            RemoteDMATransfer(dst_ids=[DstId(rid=ra, pnc=pa)], dma_engine_mask=0x0F, remote_sem=T.sem.c0,
-                              src=T.l1[0], dst=T.l1[0]),
-            RemoteDMATransfer(dst_ids=[DstId(rid=rb, pnc=pb)], dma_engine_mask=0xF0, remote_sem=T.sem.c1,
-                              src=T.l1[1], dst=T.l1[1]),
-        ], local_sem=T.sem.sent)
-        g.wait_ge(T.sem.sent, 8)
-
-    elif core == relay_a or core == relay_b:
-        t, sem = (0, T.sem.c0) if core == relay_a else (1, T.sem.c1)
-        rid, pid = topo.addr(root, core)
-        g.wait_ge(sem, 4)
-        g.remote_dma(T.l1[t], T.l1[t], sem, T.sem.sent, pid, rid, OFF_CHIP)
-        g.wait_ge(T.sem.sent, 8)
-
-    elif core == root:
+    elif core == ROOT:
         g.dma_start(T.y[:, 768:1024], T.x[:, :]).then_inc(T.sem.st, 16)
         g.wait_ge(T.sem.b0, 8)
         g.dma_start(T.y[:, 512:768], T.l2[:, :]).then_inc(T.sem.st, 16)
-        g.wait_ge(T.sem.a0, 8)
-        g.dma_start(T.y[0:64, 0:256], T.l0[0]).then_inc(T.sem.st, 16)
-        g.wait_ge(T.sem.a1, 8)
-        g.dma_start(T.y[64:128, 0:256], T.l0[1]).then_inc(T.sem.st, 16)
-        g.wait_ge(T.sem.c0, 8)
-        g.wait_ge(T.sem.c1, 8)
-        g.dma_start(T.y[:, 256:512], T.l1[0:2]).then_inc(T.sem.st, 16)
-        g.wait_ge(T.sem.st, 16 * 5)
+        for ways, rank, g0, ng in STORES:
+            for i in ways:
+                w = WAYS[i]
+                g.wait_ge(q[i], (first_share(i) if w[3] is None else share(w[2])) * w[2])
+            g.dma_start(T.y[g0 * G:(g0 + ng) * G, 256 * rank:256 * rank + 256],
+                        img[rank][g0:g0 + ng]).then_inc(T.sem.st, 16)
+        g.wait_ge(T.sem.st, 16 * (2 + len(STORES)))

@@ -8,23 +8,27 @@ SCRATCH = {
     "l1": ("dram", [NG, 128, 2 * G], "float32"),
     "l2": ("dram", [128, 256], "float32"),
 }
-SEMAPHORES = ["ld", "st", "sent", "b0", "q0", "q1", "q2", "q3", "q4", "q5", "q6", "q7"]
+SEMAPHORES = ["ld", "st", "sent", "b0", "q0", "q1", "q2", "q3", "q4", "q5", "q6", "q7", "q8", "q9"]
 
 R0, R1, R2, ROOT = 114, 242, 370, 498
 H01, H45, H67 = R0 - 2, R0 + 2, R0 + 4
 RA = R2 + 4
 
 WAYS = [
-    (0, 0, 4, None),
-    (0, 4, 3, H67),
-    (0, 7, 1, H45),
+    (0, 0, 2, None),
+    (0, 2, 2, H67),
+    (0, 4, 2, H45),
+    (0, 6, 2, H01),
     (1, 0, 3, RA),
-    (1, 3, 3, H01),
-    (1, 6, 2, H45),
+    (1, 3, 2, R0),
+    (1, 5, 1, H67),
+    (1, 6, 1, H45),
+    (1, 7, 1, H01),
 ]
+FIRST = {0: 2, 1: 1}
 STORES = [
-    ([2, 0, 1], 0, 0, 8),
-    ([5, 3, 4], 1, 0, 8),
+    ([0, 1, 2, 3], 0, 0, 8),
+    ([4, 5, 6, 7, 8], 1, 0, 8),
 ]
 
 
@@ -33,73 +37,52 @@ def share(n):
 
 
 def rank_program(g, core, T, topo):
-    q = [T.sem.q0, T.sem.q1, T.sem.q2, T.sem.q3, T.sem.q4, T.sem.q5, T.sem.q6, T.sem.q7]
+    q = [T.sem.q0, T.sem.q1, T.sem.q2, T.sem.q3, T.sem.q4, T.sem.q5, T.sem.q6, T.sem.q7, T.sem.q8, T.sem.q9]
     img = [T.l0, T.l1]
 
-    def transfers(ways, dst_of, base):
-        n = sum(WAYS[i][2] for i in ways)
-        per = share(n)
-        out, e = [], base
+    def transfers(ways, to_root, per):
+        out, e = [], 0
         for i in ways:
             rank, g0, ng, relay = WAYS[i]
-            rid, pid = topo.addr(dst_of(i), core)
+            rid, pid = topo.addr(ROOT if to_root or relay is None else relay, core)
             for k in range(g0, g0 + ng):
                 out.append(RemoteDMATransfer(dst_ids=[DstId(rid=rid, pnc=pid)], dma_engine_mask=((1 << per) - 1) << e,
                                              remote_sem=q[i], src=img[rank][k], dst=img[rank][k]))
                 e += per
-        return out, per
+        return out
 
-    def first_hop(i):
-        return WAYS[i][3] if WAYS[i][3] is not None else ROOT
-
-    def first_share(i):
-        rank = WAYS[i][0]
-        src = R0 if rank == 0 else R1
-        on = topo.mask(src, first_hop(i)) == 0xFFFF
-        return share(sum(w[2] for j, w in enumerate(WAYS)
-                         if w[0] == rank and (topo.mask(src, first_hop(j)) == 0xFFFF) == on))
-
+    sent = 0
     if core == R2:
         rid, pid = topo.addr(ROOT, core)
         g.dma_start(T.l2[:, :], T.x[:, :]).then_inc(T.sem.ld, 16)
         g.wait_ge(T.sem.ld, 16)
         g.remote_dma(T.l2[:, :], T.l2[:, :], T.sem.b0, T.sem.sent, pid, rid, 0xFF)
-        g.wait_ge(T.sem.sent, 8)
+        sent += 8
 
-    elif core == R0 or core == R1:
+    if core == R0 or core == R1:
         rank = 0 if core == R0 else 1
         mine = [i for i, w in enumerate(WAYS) if w[0] == rank]
-        off = [i for i in mine if topo.mask(core, first_hop(i)) != 0xFFFF]
-        on = [i for i in mine if topo.mask(core, first_hop(i)) == 0xFFFF]
         g.dma_start(img[rank][0:NG], T.x[:, :]).then_inc(T.sem.ld, 16)
         g.wait_ge(T.sem.ld, 16)
-        tr, per = transfers(off, first_hop, 0)
-        total = per * len(tr)
-        if on:
-            tr2, per2 = transfers(on, first_hop, 8)
-            total += per2 * len(tr2)
-            tr = tr2 + tr
-        g.remote_dma_fused(tr, local_sem=T.sem.sent)
-        g.wait_ge(T.sem.sent, total)
+        g.remote_dma_fused(transfers(mine, False, FIRST[rank]), local_sem=T.sem.sent)
+        sent += FIRST[rank] * NG
 
-    elif core in (H01, H45, H67, RA):
-        total = 0
-        for i, w in enumerate(WAYS):
-            if w[3] == core:
-                g.wait_ge(q[i], first_share(i) * w[2])
-                tr, per = transfers([i], lambda j: ROOT, 0)
-                g.remote_dma_fused(tr, local_sem=T.sem.sent)
-                total += per * len(tr)
-        g.wait_ge(T.sem.sent, total)
+    for i, w in enumerate(WAYS):
+        if w[3] == core:
+            g.wait_ge(q[i], FIRST[w[0]] * w[2])
+            g.remote_dma_fused(transfers([i], True, share(w[2])), local_sem=T.sem.sent)
+            sent += share(w[2]) * w[2]
+    if sent:
+        g.wait_ge(T.sem.sent, sent)
 
-    elif core == ROOT:
+    if core == ROOT:
         g.dma_start(T.y[:, 768:1024], T.x[:, :]).then_inc(T.sem.st, 16)
         g.wait_ge(T.sem.b0, 8)
         g.dma_start(T.y[:, 512:768], T.l2[:, :]).then_inc(T.sem.st, 16)
         for ways, rank, g0, ng in STORES:
             for i in ways:
                 w = WAYS[i]
-                g.wait_ge(q[i], (first_share(i) if w[3] is None else share(w[2])) * w[2])
+                g.wait_ge(q[i], (FIRST[w[0]] if w[3] is None else share(w[2])) * w[2])
             g.dma_start(T.y[g0 * G:(g0 + ng) * G, 256 * rank:256 * rank + 256],
                         img[rank][g0:g0 + ng]).then_inc(T.sem.st, 16)
         g.wait_ge(T.sem.st, 16 * (2 + len(STORES)))

@@ -8,7 +8,7 @@ SCRATCH = {
     "l1": ("dram", [NG, 128, 2 * G], "float32"),
     "l2": ("dram", [128, 256], "float32"),
 }
-SEMAPHORES = ["ld", "st", "sent", "b0", "q0", "q1", "q2", "q3", "q4", "q5", "q6", "q7", "q8", "q9"]
+SEMAPHORES = ["ld", "st", "sent", "b0", "q0", "q1", "q2", "q3", "q4", "q5", "q6", "q7", "q8"]
 
 R0, R1, R2, ROOT = 114, 242, 370, 498
 H01, H45, H67 = R0 - 2, R0 + 2, R0 + 4
@@ -37,7 +37,7 @@ def share(n):
 
 
 def rank_program(g, core, T, topo):
-    q = [T.sem.q0, T.sem.q1, T.sem.q2, T.sem.q3, T.sem.q4, T.sem.q5, T.sem.q6, T.sem.q7, T.sem.q8, T.sem.q9]
+    q = [T.sem.q0, T.sem.q1, T.sem.q2, T.sem.q3, T.sem.q4, T.sem.q5, T.sem.q6, T.sem.q7, T.sem.q8]
     img = [T.l0, T.l1]
 
     def transfers(ways, to_root, per):

from concourse.bass import RemoteDMATransfer, DstId

G = 16
NG = 128 // G

SCRATCH = {
    "l0": ("dram", [NG, 128, 2 * G], "float32"),
    "l1": ("dram", [NG, 128, 2 * G], "float32"),
    "l2": ("dram", [128, 256], "float32"),
}
SEMAPHORES = ["ld", "st", "sent", "b0", "q0", "q1", "q2", "q3", "q4", "q5", "q6", "q7", "q8"]

R0, R1, R2, ROOT = 114, 242, 370, 498
H01, H45, H67 = R0 - 2, R0 + 2, R0 + 4
RA = R2 + 4

WAYS = [
    (0, 0, 2, None),
    (0, 2, 2, H67),
    (0, 4, 2, H45),
    (0, 6, 2, H01),
    (1, 0, 3, RA),
    (1, 3, 2, R0),
    (1, 5, 1, H67),
    (1, 6, 1, H45),
    (1, 7, 1, H01),
]
FIRST = {0: 2, 1: 1}
STORES = [
    ([0, 1, 2, 3], 0, 0, 8),
    ([4, 5, 6, 7, 8], 1, 0, 8),
]


def share(n):
    return {1: 8, 2: 4, 3: 2, 4: 2}.get(n, 1)


def rank_program(g, core, T, topo):
    q = [T.sem.q0, T.sem.q1, T.sem.q2, T.sem.q3, T.sem.q4, T.sem.q5, T.sem.q6, T.sem.q7, T.sem.q8]
    img = [T.l0, T.l1]

    def transfers(ways, to_root, per):
        out, e = [], 0
        for i in ways:
            rank, g0, ng, relay = WAYS[i]
            rid, pid = topo.addr(ROOT if to_root or relay is None else relay, core)
            for k in range(g0, g0 + ng):
                out.append(RemoteDMATransfer(dst_ids=[DstId(rid=rid, pnc=pid)], dma_engine_mask=((1 << per) - 1) << e,
                                             remote_sem=q[i], src=img[rank][k], dst=img[rank][k]))
                e += per
        return out

    sent = 0
    if core == R2:
        rid, pid = topo.addr(ROOT, core)
        g.dma_start(T.l2[:, :], T.x[:, :]).then_inc(T.sem.ld, 16)
        g.wait_ge(T.sem.ld, 16)
        g.remote_dma(T.l2[:, :], T.l2[:, :], T.sem.b0, T.sem.sent, pid, rid, 0xFF)
        sent += 8

    if core == R0 or core == R1:
        rank = 0 if core == R0 else 1
        mine = [i for i, w in enumerate(WAYS) if w[0] == rank]
        g.dma_start(img[rank][0:NG], T.x[:, :]).then_inc(T.sem.ld, 16)
        g.wait_ge(T.sem.ld, 16)
        g.remote_dma_fused(transfers(mine, False, FIRST[rank]), local_sem=T.sem.sent)
        sent += FIRST[rank] * NG

    for i, w in enumerate(WAYS):
        if w[3] == core:
            g.wait_ge(q[i], FIRST[w[0]] * w[2])
            g.remote_dma_fused(transfers([i], True, share(w[2])), local_sem=T.sem.sent)
            sent += share(w[2]) * w[2]
    if sent:
        g.wait_ge(T.sem.sent, sent)

    if core == ROOT:
        g.dma_start(T.y[:, 768:1024], T.x[:, :]).then_inc(T.sem.st, 16)
        g.wait_ge(T.sem.b0, 8)
        g.dma_start(T.y[:, 512:768], T.l2[:, :]).then_inc(T.sem.st, 16)
        for ways, rank, g0, ng in STORES:
            for i in ways:
                w = WAYS[i]
                g.wait_ge(q[i], (FIRST[w[0]] if w[3] is None else share(w[2])) * w[2])
            g.dma_start(T.y[g0 * G:(g0 + ng) * G, 256 * rank:256 * rank + 256],
                        img[rank][g0:g0 + ng]).then_inc(T.sem.st, 16)
        g.wait_ge(T.sem.st, 16 * (2 + len(STORES)))
